import numpy as np
import ml_dtypes


def mxq(x, axis, fmt="e4m3"):
    dtype, down = {"e4m3": (ml_dtypes.float8_e4m3fn, 7), "e5m2": (ml_dtypes.float8_e5m2, 14)}[fmt]
    v = np.moveaxis(np.asarray(x, np.float32).astype(ml_dtypes.bfloat16).astype(np.float64), axis, -1)
    blocks = v.reshape(v.shape[:-1] + (-1, 32))
    amax = np.abs(blocks).max(-1, keepdims=True)
    byte = np.maximum(np.where(amax > 0, np.frexp(amax)[1] - 1 + 127, 0) - down, 1)
    scale = np.exp2(byte - 127.0)
    codes = (blocks / scale).astype(np.float32).astype(dtype).astype(np.float64)
    return np.moveaxis((codes * scale).reshape(v.shape), -1, axis)


WIDE = False


def mx_kscale(k):
    if not WIDE:
        return np.ones(k)
    levels = np.array([10, -10, 5, -5, 0])
    if k % 512:
        return np.exp2(np.random.permutation(np.resize(levels, k // 32))).repeat(32)
    a = np.empty((k // 512, 16))
    for p in range(k // 512):
        a[p, :8] = np.random.permutation(np.resize(levels, 8))
        for g in range(8):
            far = levels[np.abs(levels - a[p, g]) >= 10]
            a[p, g + 8] = far[np.random.randint(len(far))]
    return np.exp2(a.ravel()).repeat(32)


def f64(x):
    return np.asarray(x).astype(np.float64)


def striped(idx):
    return np.tile(idx.reshape(-1, 16).T, (8, 1)).astype(np.uint16)


def unstriped(offs):
    return offs[:16].T.reshape(-1).astype(np.int64)


E2M1 = np.array([0.0, 0.5, 1.0, 1.5, 2.0, 3.0, 4.0, 6.0, -0.0, -0.5, -1.0, -1.5, -2.0, -3.0, -4.0, -6.0])


def pack_weight(w, fmt):
    k, n = w.shape
    w = f64(np.asarray(w, np.float32).astype(ml_dtypes.bfloat16)).reshape(k // 32, 32, n)
    amax = np.abs(w).max(1)
    if fmt == "e4m3":
        byte = np.frexp(amax)[1] - 1 + 127 - 7
    else:
        mant, ex = np.frexp(amax / 6.0)
        byte = np.where(mant > 0.5, ex, ex - 1) + 127
    byte = np.clip(np.where(amax > 0, byte, 1), 1, 254)
    scaled = (w * np.exp2(127.0 - byte)[:, None, :]).reshape(k, n).astype(np.float32)
    by_word = np.ascontiguousarray(scaled.reshape(k // 512, 128, 4, n).transpose(0, 1, 3, 2))
    if fmt == "e4m3":
        words = by_word.astype(ml_dtypes.float8_e4m3fn).view(np.uint8)
    else:
        c = by_word.astype(ml_dtypes.float4_e2m1fn).view(np.uint8) & 0xF
        words = (c[..., 0::2] | (c[..., 1::2] << 4)).reshape(k // 512, 128, 2 * n)
    return np.ascontiguousarray(words), np.ascontiguousarray(byte.astype(np.uint8).reshape(k // 512, 16, n))


def unpack_weight(words, scales, fmt):
    g, _, n = scales.shape
    words = np.ascontiguousarray(words).reshape(g, 128, n, -1)
    if fmt == "e4m3":
        vals = words.view(ml_dtypes.float8_e4m3fn).astype(np.float64)
    else:
        nib = np.empty((g, 128, n, 4), np.uint8)
        nib[..., 0::2] = words & 0xF
        nib[..., 1::2] = words >> 4
        vals = E2M1[nib]
    vals = vals * np.repeat(np.exp2(scales.astype(np.float64) - 127.0), 8, axis=1)[..., None]
    return vals.transpose(0, 1, 3, 2).reshape(g * 512, n)


def gelu(v):
    return 0.5 * v * (1.0 + np.tanh(np.sqrt(2.0 / np.pi) * (v + 0.044715 * v**3)))


def striped8(idx):
    return np.concatenate([v.reshape(-1, 16).T for v in idx]).astype(np.uint16)


def unstriped8(offs):
    return np.stack([offs[16 * g:16 * g + 16].T.reshape(-1) for g in range(8)]).astype(np.int64)


def put_heads(h, wgs, idx8, t2):
    r = np.arange(h.shape[0])
    page = np.zeros((h.shape[0], t2))
    page[r[:, None], idx8[r % 512 // 64]] = wgs[r // 4 % 128] * h
    return page


def bf(x):
    return np.asarray(x, np.float32).astype(ml_dtypes.bfloat16)


def planes(Y):
    n, m = Y.shape
    b = f64(bf(Y)).reshape(n // 32, 32, m)
    amax = np.abs(b).max(1)
    byte = np.clip(np.where(amax > 0, np.frexp(amax)[1] - 1 + 127 - 7, 1), 1, 254)
    codes = (b * np.exp2(127.0 - byte)[:, None, :]).reshape(n, m).astype(np.float32).astype(ml_dtypes.float8_e4m3fn).view(np.uint8)
    words = codes.reshape(n // 512, 128, 4, m).transpose(0, 1, 3, 2)
    return np.ascontiguousarray(words), np.ascontiguousarray(byte.astype(np.uint8).reshape(n // 512, 16, m))


K, T, S, H, T2, P, N = 1024, 2048, 512, 1024, 1024, 512, 512

def setup_inputs():
    n = np.random.standard_normal
    s = mx_kscale(K)[:, None]
    u = mx_kscale(H)[:, None]
    tab_words, tab_scales = pack_weight(n((K, T)) * s, "e4m3")
    w2_words, w2_scales = pack_weight(2.5 * n((K, H)) / np.sqrt(K) / s, "e2m1")
    w4_words, w4_scales = pack_weight(n((H, N)) / np.sqrt(H) * np.exp(0.8 * n(N)) / u, "e4m3")
    return {
        "tab_words": tab_words, "tab_scales": tab_scales,
        "offs": striped(np.random.permutation(T)[:S]),
        "w1": (0.09 * n((K, H)) / np.sqrt(K) / s).astype(np.float32),
        "w2_words": w2_words, "w2_scales": w2_scales,
        "w3": (0.56 * n((K, H)) / np.sqrt(K) / s).astype(np.float32),
        "amp": np.random.uniform(0.15, 0.26, H).astype(np.float32),
        "wgs": np.repeat(np.random.uniform(0.5, 2.0, (8, S)), 16, axis=0).astype(np.float32),
        "offs2": striped8(np.stack([np.random.permutation(T2)[:S] for _ in range(8)])),
        "offs3": striped(np.random.permutation(T2)[:P]),
        "geo": (n((H, P)) * u).astype(np.float32),
        "w4_words": w4_words, "w4_scales": w4_scales,
    }

def reference(tab_words, tab_scales, offs, w1, w2_words, w2_scales, w3, amp, wgs, offs2, offs3, geo, w4_words, w4_scales):
    v = unpack_weight(tab_words, tab_scales, "e4m3")[:, unstriped(offs)]
    W1 = mxq(f64(w1), 0, "e4m3")
    W2 = unpack_weight(w2_words, w2_scales, "e2m1")
    W3 = mxq(f64(w3), 0, "e4m3")
    a = W1.T @ v
    b = np.tanh(W2.T @ v)
    d = np.sin(W3.T @ v)
    h = a + f64(amp)[:, None] * b + d
    page = put_heads(h, f64(wgs), unstriped8(offs2), T2)
    x = page[:, unstriped(offs3)]
    z = mxq(f64(geo) * np.cos(x), 0, "e4m3")
    W4 = unpack_weight(w4_words, w4_scales, "e4m3")
    y = W4.T @ z
    words, scales = planes(y)
    return y, words, scales

@@ -1,0 +1,294 @@
+import math
+from contextlib import ExitStack
+
+import concourse.mybir as mybir
+from concourse.masks import make_identity
+
+K, T, S, H, T2, M, N = 1024, 2048, 512, 1024, 1024, 512, 512
+FLOPS = 2 * (3 * K * H * S + H * N * M)
+
+F32 = mybir.dt.float32
+BF16 = mybir.dt.bfloat16
+I32 = mybir.dt.int32
+U32 = mybir.dt.uint32
+U16 = mybir.dt.uint16
+U8 = mybir.dt.uint8
+FP8X4 = mybir.dt.float8_e4m3fn_x4
+FP4X4 = mybir.dt.float4_e2m1fn_x4
+ACT = mybir.ActivationFunctionType
+MULT = mybir.AluOpType.mult
+
+P = 128
+PACK = 4
+PASS = P * PACK
+QUADS = 4
+
+
+def tile_list_vibrometer_slot_features_kernel(
+    tc, tab_words, tab_scales, offs, w1, w2_words, w2_scales, w3, amp, wgs, offs2, offs3, geo,
+    w4_words, w4_scales, out_0, out_1, out_2,
+):
+    nc = tc.nc
+    with ExitStack() as ctx:
+        keep = ctx.enter_context(tc.tile_pool(name="keep", bufs=1))
+        big = ctx.enter_context(tc.tile_pool(name="big", bufs=7))
+        ring = ctx.enter_context(tc.tile_pool(name="ring", bufs=3))
+        psum = ctx.enter_context(tc.psum_pool(name="psum", bufs=2))
+
+        list1 = keep.tile([P, S // 16], U16, name="list1")
+        list2 = keep.tile([P, S // 16], U16, name="list2")
+        list3 = keep.tile([P, M // 16], U16, name="list3")
+        tab_s = keep.tile([P, 2 * T], U8, name="tab_s", align_bytes=64)
+        w2_s = keep.tile([P, 2 * H], U8, name="w2_s", align_bytes=64)
+        w4_s = keep.tile([P, N], U8, name="w4_s", align_bytes=64)
+        nc.vector.memset(tab_s[:].bitcast(I32), 0)
+        nc.vector.memset(w2_s[:].bitcast(I32), 0)
+        nc.vector.memset(w4_s[:].bitcast(I32), 0)
+        pages = [keep.tile([P, T2], F32, name="page%d" % n) for n in range(2)]
+        for page in pages:
+            nc.vector.memset(page[:], 0.0)
+        ident = keep.tile([P, P], F32, name="ident")
+        make_identity(nc, ident[:])
+
+        nc.sync.dma_start(list1[:], offs)
+        tab_w = [keep.tile([P, T], I32, name="tab_w%d" % a, align_bytes=64) for a in range(2)]
+
+        def load_scales(dst, src):
+            for q in range(QUADS):
+                nc.sync.dma_start(
+                    dst[32 * q:32 * q + 4, :].bitcast(I32).rearrange("r (a n) -> r a n", a=2),
+                    src[:, 4 * q:4 * q + 4, :].bitcast(I32).rearrange("a r n -> r a n"),
+                )
+
+        def load_chunk(w, b, a, pieces=1):
+            raw = big.tile([P, PACK, PASS], F32, name="raw", tag="big")
+            rows = w[PASS * a:PASS * (a + 1), PASS * b:PASS * (b + 1)].rearrange("(p t) c -> p t c", t=PACK)
+            width = PASS // pieces
+            for lo in range(0, PASS, width):
+                nc.sync.dma_start(raw[:, :, lo:lo + width], rows[:, :, lo:lo + width])
+            return raw
+
+        def load_table(a):
+            nc.sync.dma_start(tab_w[a][:], tab_words[a].rearrange("p t i -> p (t i)").bitcast(I32))
+
+        raws = {}
+        raws["w1", 0, 0] = load_chunk(w1, 0, 0)
+        load_scales(tab_s, tab_scales)
+        load_table(0)
+        w2_w = keep.tile([P, 2, 2 * H], U8, name="w2_w", align_bytes=64)
+        nc.sync.dma_start(w2_w[:].bitcast(I32), w2_words.bitcast(I32).rearrange("a p n -> p a n"))
+        amp_col = keep.tile([P, 2, PACK], F32, name="amp_col")
+        nc.sync.dma_start(amp_col[:], amp.rearrange("(b q i) -> q b i", b=2, i=PACK))
+        load_table(1)
+        load_scales(w2_s, w2_scales)
+        raws["w1", 0, 1] = load_chunk(w1, 0, 1)
+        raws["w3", 0, 0] = load_chunk(w3, 0, 0)
+        raws["w3", 0, 1] = load_chunk(w3, 0, 1, 2)
+        wgs_sb = keep.tile([P, S], F32, name="wgs_sb")
+        nc.sync.dma_start(list2[:], offs2)
+        nc.sync.dma_start(wgs_sb[:], wgs)
+        nc.sync.dma_start(list3[:], offs3)
+        w4_w = keep.tile([P, 2, N], I32, name="w4_w", align_bytes=64)
+        nc.sync.dma_start(w4_w[:], w4_words.rearrange("a p c i -> p a (c i)").bitcast(I32))
+        for q in range(QUADS):
+            nc.sync.dma_start(
+                w4_s[32 * q:32 * q + 8, :].bitcast(I32), w4_scales[:, 4 * q:4 * q + 4, :].bitcast(I32))
+        for name, w in (("w1", w1), ("w3", w3)):
+            for a in range(2):
+                raws[name, 1, a] = load_chunk(w, 1, a)
+        geo_sb = []
+        for b in range(2):
+            g = big.tile([P, PACK, M], F32, name="geo%d" % b, tag="big")
+            nc.sync.dma_start(g[:], geo[PASS * b:PASS * (b + 1), :].rearrange("(p t) m -> p t m", t=PACK))
+            geo_sb.append(g)
+
+        v_s = [keep.tile([P, S], U8, name="v_s%d" % a, align_bytes=64) for a in range(2)]
+        v_w = [keep.tile([P, S], U32, name="v_w%d" % a, align_bytes=64) for a in range(2)]
+        for a in range(2):
+            nc.vector.tensor_copy(v_s[a][:], tab_s[:, T * a:T * (a + 1)].indirect(list1[:]))
+        for a in range(2):
+            nc.vector.tensor_copy(v_w[a][:], tab_w[a][:].bitcast(U32).indirect(list1[:]))
+
+        amp_row = []
+        for b in range(2):
+            bank = psum.tile([P, PASS], F32, name="amp_row", tag="amp")
+            for i in range(PACK):
+                nc.tensor.transpose(bank[:, P * i:P * (i + 1)], amp_col[:, b, i:i + 1].to_broadcast([P, P]), ident[:])
+            amp_row.append(bank)
+
+        tanhs = [keep.tile([P, PACK, 4, P], F32, name="tanh%d" % b) for b in range(2)]
+        limited = [tanhs[0][:], raws["w3", 0, 1][:].rearrange("p i (j q) -> p i j q", j=4)]
+
+        def limited_features(b):
+            banks = [psum.tile([P, PASS], F32, name="bank", tag="mx", bufs=4) for jb in range(4)]
+            for a in range(2):
+                for jb in range(4):
+                    cols = slice(P * jb, P * (jb + 1))
+                    nc.tensor.matmul_mx(
+                        out=banks[jb][:], lhsT=v_w[a][:, cols].bitcast(FP8X4), lhsT_scale=v_s[a][:, cols],
+                        rhs=w2_w[:, a, 2 * PASS * b:2 * PASS * (b + 1)].bitcast(FP4X4),
+                        rhs_scale=w2_s[:, H * a + PASS * b:H * a + PASS * (b + 1)],
+                        start=(a == 0), stop=(a == 1))
+            for jb, bank in enumerate(banks):
+                nc.scalar.activation(tanhs[b][:, :, jb, :], bank[:].rearrange("p (q i) -> p i q", i=PACK), ACT.Tanh)
+                nc.vector.tensor_tensor(
+                    limited[b][:, :, jb, :], tanhs[b][:, :, jb, :], amp_row[b][:].rearrange("p (i q) -> p i q", i=PACK), MULT)
+
+        codes, scales = {}, {}
+
+        def quantise_chunk(key, shares, cuts=(0, PACK)):
+            raw = raws[key]
+            grouped = ring.tile([P, PACK, P, PACK], BF16, name="grouped", align_bytes=64)
+            dst = grouped[:].rearrange("p i q t -> p q t i")
+            src = raw[:].rearrange("p t (q i) -> p q t i", i=PACK)
+            for engine, lo, hi in shares:
+                if engine == "vector":
+                    nc.vector.tensor_copy(dst[:, lo:hi], src[:, lo:hi])
+                else:
+                    nc.scalar.copy(dst[:, lo:hi], src[:, lo:hi])
+            label = "%s%d%d" % key
+            codes[key] = keep.tile([P, PASS], U32, name="c" + label, align_bytes=64)
+            scales[key] = keep.tile([P, PASS], U8, name="s" + label, align_bytes=64)
+            for lo, hi in zip(cuts, cuts[1:]):
+                nc.vector.quantize_mx(
+                    out=codes[key][:, P * lo:P * hi].bitcast(FP8X4), scales=scales[key][:, P * lo:P * hi],
+                    in_=grouped[:, lo:hi].rearrange("p i q t -> p (i q t)"))
+
+        def product(name, b, i):
+            bank = psum.tile([P, PASS], F32, name="bank", tag="mx", bufs=4)
+            rows = slice(P * i, P * (i + 1))
+            for a in range(2):
+                for jb in range(4):
+                    cols = slice(P * jb, P * (jb + 1))
+                    nc.tensor.matmul_mx(
+                        out=bank[:, cols], lhsT=v_w[a][:, cols].bitcast(FP8X4), lhsT_scale=v_s[a][:, cols],
+                        rhs=codes[name, b, a][:, rows].bitcast(FP8X4), rhs_scale=scales[name, b, a][:, rows],
+                        start=(a == 0 and jb == 0), stop=(a == 1 and jb == 3))
+            return bank
+
+        def features(n):
+            b, i = divmod(n, PACK)
+            plain = ring.tile([P, PASS], F32, name="plain")
+            nc.scalar.copy(plain[:], product("w1", b, i)[:])
+            phase = ring.tile([P, PASS], F32, name="phase")
+            nc.scalar.activation(phase[:], product("w3", b, i)[:], ACT.Sin)
+            bank = psum.tile([P, S], F32, name="hsum", tag="hsum")
+            terms = (limited[b][:, i].rearrange("p j q -> p (j q)"), plain[:], phase[:])
+            for k, term in enumerate(terms):
+                for jb in range(4):
+                    cols = slice(P * jb, P * (jb + 1))
+                    nc.tensor.matmul(
+                        bank[:, cols], term[:, cols], ident[:], start=(k == 0 and jb == 0), stop=(k == 2 and jb == 3),
+                        is_transpose=True)
+            if n in (2, 3):
+                h = raws[("w1", "w3")[n - 2], 1, 1][:, 0, :]
+            else:
+                h = ring.tile([P, S], F32, name="h")[:]
+            nc.scalar.copy(h, bank[:])
+            return h
+
+        cos_x = [keep.tile([P, PACK, M], F32, name="cos_x%d" % b) for b in range(2)]
+
+        def put(n, h):
+            nc.vector.tensor_tensor(pages[n % 2][:].indirect(list2[:]), h, wgs_sb[:], MULT)
+
+        def pick(n, lo, hi):
+            b, i = divmod(n, PACK)
+            nc.vector.tensor_copy(cos_x[b][:, i, lo:hi], pages[n % 2][:].indirect(list3[:, lo // 16:hi // 16]))
+
+        def cosine(n, lo, hi):
+            b, i = divmod(n, PACK)
+            size = limited[1][:, min(max(n - 1, 0), 3)].rearrange("p j q -> p (j q)")[:, lo:hi]
+            nc.scalar.activation(size, cos_x[b][:, i, lo:hi], ACT.Abs)
+            nc.scalar.activation(cos_x[b][:, i, lo:hi], size, ACT.Sin, bias=math.pi / 2, scale=-1.0)
+
+        z_w = [keep.tile([P, M], U32, name="z_w%d" % b, align_bytes=64) for b in range(2)]
+        z_s = [keep.tile([P, M], U8, name="z_s%d" % b, align_bytes=64) for b in range(2)]
+
+        def quantise_z(b, lo, hi):
+            z = ring.tile([P, hi - lo, PACK], BF16, name="z", align_bytes=64, bufs=2)
+            nc.vector.tensor_tensor(
+                z[:].rearrange("p (c i) t -> p c t i", i=4),
+                cos_x[b][:, :, lo:hi].rearrange("p t (c i) -> p c t i", i=4),
+                geo_sb[b][:, :, lo:hi].rearrange("p t (c i) -> p c t i", i=4), MULT)
+            nc.vector.quantize_mx(
+                out=z_w[b][:, lo:hi].bitcast(FP8X4), scales=z_s[b][:, lo:hi], in_=z[:].rearrange("p m t -> p (m t)"))
+
+        w4_wd = keep.tile([P, 2, N], I32, name="w4_wd", align_bytes=64)
+        w4_sd = keep.tile([P, N], U8, name="w4_sd", align_bytes=64)
+
+        def deal_w4():
+            nc.vector.tensor_copy(
+                w4_wd[:].rearrange("p a (t q) -> p a q t", t=PACK), w4_w[:].rearrange("p a (q t) -> p a q t", t=PACK))
+            nc.vector.tensor_copy(
+                w4_sd[:].rearrange("p (t q) -> p q t", t=PACK), w4_s[:].rearrange("p (q t) -> p q t", t=PACK))
+
+        y_banks = {}
+
+        def project(b, mq):
+            if b == 0:
+                y_banks[mq] = psum.tile([P, PACK, P], F32, name="bank", tag="mx", bufs=4)
+            cols = slice(P * mq, P * (mq + 1))
+            for t in range(PACK):
+                rows = slice(P * t, P * (t + 1))
+                nc.tensor.matmul_mx(
+                    out=y_banks[mq][:, t, :], lhsT=w4_wd[:, b, rows].bitcast(FP8X4), lhsT_scale=w4_sd[4 * b:P, rows],
+                    rhs=z_w[b][:, cols].bitcast(FP8X4), rhs_scale=z_s[b][:, cols],
+                    start=(b == 0 and t == 0), stop=(b == 1 and t == PACK - 1))
+
+        y_w = keep.tile([P, M], I32, name="y_w", align_bytes=64)
+        y_s = keep.tile([P, M], U8, name="y_s", align_bytes=64)
+        out_rows = out_0.rearrange("(p t) m -> p t m", t=PACK)
+        out_words = out_1[0].rearrange("p m t -> p (m t)").bitcast(I32)
+
+        def hand_out(mq):
+            cols = slice(P * mq, P * (mq + 1))
+            y = ring.tile([P, PACK, P], F32, name="y", bufs=4)
+            nc.scalar.copy(y[:], y_banks[mq][:])
+            nc.sync.dma_start(out_rows[:, :, cols], y[:])
+            y_bf = ring.tile([P, P, PACK], BF16, name="y_bf", align_bytes=64, bufs=2)
+            nc.vector.tensor_copy(
+                y_bf[:].rearrange("p (c i) t -> p c t i", i=4), y[:].rearrange("p t (c i) -> p c t i", i=4))
+            nc.vector.quantize_mx(
+                out=y_w[:, cols].bitcast(FP8X4), scales=y_s[:, cols], in_=y_bf[:].rearrange("p m t -> p (m t)"))
+            nc.sync.dma_start(out_words[:, cols], y_w[:, cols])
+
+        quantise_chunk(("w1", 0, 0), [("scalar", 0, P)])
+        limited_features(0)
+        quantise_chunk(("w1", 0, 1), [("vector", 0, P)])
+        quantise_chunk(("w3", 0, 0), [("vector", 0, P)])
+        quantise_chunk(("w3", 0, 1), [("vector", 0, P // 2), ("vector", P // 2, P)], (0, 1, PACK))
+        limited_features(1)
+        second = [("w1", 1, 0), ("w1", 1, 1), ("w3", 1, 0), ("w3", 1, 1)]
+        hs = {0: features(0)}
+        deal_w4()
+        for n in range(8):
+            if n in (1, 2):
+                quantise_chunk(second[2 * n - 2], [("scalar", 0, P)])
+                quantise_chunk(second[2 * n - 1], [("scalar", 0, P)])
+            if n + 1 < 8:
+                hs[n + 1] = features(n + 1)
+            if n == 3:
+                cosine(0, 0, M)
+            if n >= 3 and n < 6:
+                cosine(n - 2, 0, M)
+            if n == 5:
+                quantise_z(0, 0, M)
+            put(n, hs[n])
+            if n < 7:
+                pick(n, 0, M)
+        for n in range(4, 7):
+            cosine(n, 0, M)
+        for mq in range(4):
+            project(0, mq)
+        for half in range(2):
+            pick(7, 256 * half, 256 * (half + 1))
+            cosine(7, 256 * half, 256 * (half + 1))
+        for half in range(2):
+            quantise_z(1, 256 * half, 256 * (half + 1))
+            for mq in (2 * half, 2 * half + 1):
+                project(1, mq)
+        for mq in range(4):
+            hand_out(mq)
+        for q in range(QUADS):
+            nc.scalar.dma_start(out_2[0, 4 * q:4 * q + 4, :].bitcast(I32), y_s[32 * q:32 * q + 4, :].bitcast(I32))

@@ -22,6 +22,7 @@ P = 128
 PACK = 4
 PASS = P * PACK
 QUADS = 4
+PAGES = 3
 
 
 def tile_list_vibrometer_slot_features_kernel(
@@ -44,7 +45,7 @@ def tile_list_vibrometer_slot_features_kernel(
         nc.vector.memset(tab_s[:].bitcast(I32), 0)
         nc.vector.memset(w2_s[:].bitcast(I32), 0)
         nc.vector.memset(w4_s[:].bitcast(I32), 0)
-        pages = [keep.tile([P, T2], F32, name="page%d" % n) for n in range(2)]
+        pages = [keep.tile([P, T2], F32, name="page%d" % n) for n in range(PAGES)]
         for page in pages:
             nc.vector.memset(page[:], 0.0)
         ident = keep.tile([P, P], F32, name="ident")
@@ -72,30 +73,30 @@ def tile_list_vibrometer_slot_features_kernel(
             nc.sync.dma_start(tab_w[a][:], tab_words[a].rearrange("p t i -> p (t i)").bitcast(I32))
 
         raws = {}
-        raws["w1", 0, 0] = load_chunk(w1, 0, 0)
-        load_scales(tab_s, tab_scales)
-        load_table(0)
-        w2_w = keep.tile([P, 2, 2 * H], U8, name="w2_w", align_bytes=64)
-        nc.sync.dma_start(w2_w[:].bitcast(I32), w2_words.bitcast(I32).rearrange("a p n -> p a n"))
         amp_col = keep.tile([P, 2, PACK], F32, name="amp_col")
         nc.sync.dma_start(amp_col[:], amp.rearrange("(b q i) -> q b i", b=2, i=PACK))
+        load_table(0)
+        load_scales(tab_s, tab_scales)
         load_table(1)
+        w2_w = keep.tile([P, 2, 2 * H], U8, name="w2_w", align_bytes=64)
+        nc.sync.dma_start(w2_w[:].bitcast(I32), w2_words.bitcast(I32).rearrange("a p n -> p a n"))
         load_scales(w2_s, w2_scales)
-        raws["w1", 0, 1] = load_chunk(w1, 0, 1)
         raws["w3", 0, 0] = load_chunk(w3, 0, 0)
-        raws["w3", 0, 1] = load_chunk(w3, 0, 1, 2)
+        raws["w3", 0, 1] = load_chunk(w3, 0, 1)
+        raws["w1", 0, 0] = load_chunk(w1, 0, 0)
+        raws["w1", 0, 1] = load_chunk(w1, 0, 1, 2)
         wgs_sb = keep.tile([P, S], F32, name="wgs_sb")
         nc.sync.dma_start(list2[:], offs2)
         nc.sync.dma_start(wgs_sb[:], wgs)
         nc.sync.dma_start(list3[:], offs3)
+        for name, w in (("w3", w3), ("w1", w1)):
+            for a in range(2):
+                raws[name, 1, a] = load_chunk(w, 1, a)
         w4_w = keep.tile([P, 2, N], I32, name="w4_w", align_bytes=64)
         nc.sync.dma_start(w4_w[:], w4_words.rearrange("a p c i -> p a (c i)").bitcast(I32))
         for q in range(QUADS):
             nc.sync.dma_start(
                 w4_s[32 * q:32 * q + 8, :].bitcast(I32), w4_scales[:, 4 * q:4 * q + 4, :].bitcast(I32))
-        for name, w in (("w1", w1), ("w3", w3)):
-            for a in range(2):
-                raws[name, 1, a] = load_chunk(w, 1, a)
         geo_sb = []
         for b in range(2):
             g = big.tile([P, PACK, M], F32, name="geo%d" % b, tag="big")
@@ -106,7 +107,6 @@ def tile_list_vibrometer_slot_features_kernel(
         v_w = [keep.tile([P, S], U32, name="v_w%d" % a, align_bytes=64) for a in range(2)]
         for a in range(2):
             nc.vector.tensor_copy(v_s[a][:], tab_s[:, T * a:T * (a + 1)].indirect(list1[:]))
-        for a in range(2):
             nc.vector.tensor_copy(v_w[a][:], tab_w[a][:].bitcast(U32).indirect(list1[:]))
 
         amp_row = []
@@ -117,12 +117,12 @@ def tile_list_vibrometer_slot_features_kernel(
             amp_row.append(bank)
 
         tanhs = [keep.tile([P, PACK, 4, P], F32, name="tanh%d" % b) for b in range(2)]
-        limited = [tanhs[0][:], raws["w3", 0, 1][:].rearrange("p i (j q) -> p i j q", j=4)]
+        limited = [tanhs[0][:], raws["w1", 0, 1][:].rearrange("p i (j q) -> p i j q", j=4)]
 
         def limited_features(b):
             banks = [psum.tile([P, PASS], F32, name="bank", tag="mx", bufs=4) for jb in range(4)]
-            for a in range(2):
-                for jb in range(4):
+            for jb in range(4):
+                for a in range(2):
                     cols = slice(P * jb, P * (jb + 1))
                     nc.tensor.matmul_mx(
                         out=banks[jb][:], lhsT=v_w[a][:, cols].bitcast(FP8X4), lhsT_scale=v_s[a][:, cols],
@@ -135,10 +135,12 @@ def tile_list_vibrometer_slot_features_kernel(
                     limited[b][:, :, jb, :], tanhs[b][:, :, jb, :], amp_row[b][:].rearrange("p (i q) -> p i q", i=PACK), MULT)
 
         codes, scales = {}, {}
+        shared = [keep.tile([P, 2 * PASS], F32, name="shared%d" % n, align_bytes=64) for n in range(4)]
 
         def quantise_chunk(key, shares, cuts=(0, PACK)):
             raw = raws[key]
-            grouped = ring.tile([P, PACK, P, PACK], BF16, name="grouped", align_bytes=64)
+            place = shared[2 * (key[0] == "w1") + key[2]]
+            grouped = place[:].bitcast(BF16).rearrange("p (i q t) -> p i q t", i=PACK, t=PACK)
             dst = grouped[:].rearrange("p i q t -> p q t i")
             src = raw[:].rearrange("p t (q i) -> p q t i", i=PACK)
             for engine, lo, hi in shares:
@@ -166,47 +168,64 @@ def tile_list_vibrometer_slot_features_kernel(
                         start=(a == 0 and jb == 0), stop=(a == 1 and jb == 3))
             return bank
 
+        spent = {}
+
+        def limited_slice(n):
+            return limited[n // PACK][:, n % PACK].rearrange("p j q -> p (j q)")
+
         def features(n):
+            return features_end(n, features_start(n))
+
+        def features_start(n):
             b, i = divmod(n, PACK)
-            plain = ring.tile([P, PASS], F32, name="plain")
-            nc.scalar.copy(plain[:], product("w1", b, i)[:])
             phase = ring.tile([P, PASS], F32, name="phase")
+            plain = shared[n][:, 0:PASS] if n < PACK else ring.tile([P, PASS], F32, name="plain")
+            spent[n] = (phase, plain)
             nc.scalar.activation(phase[:], product("w3", b, i)[:], ACT.Sin)
+            nc.scalar.copy(plain[:], product("w1", b, i)[:])
             bank = psum.tile([P, S], F32, name="hsum", tag="hsum")
-            terms = (limited[b][:, i].rearrange("p j q -> p (j q)"), plain[:], phase[:])
+            terms = (limited_slice(n), phase[:], plain[:]) if n % PACK < 2 else (phase[:], plain[:], limited_slice(n))
             for k, term in enumerate(terms):
                 for jb in range(4):
                     cols = slice(P * jb, P * (jb + 1))
                     nc.tensor.matmul(
                         bank[:, cols], term[:, cols], ident[:], start=(k == 0 and jb == 0), stop=(k == 2 and jb == 3),
                         is_transpose=True)
-            if n in (2, 3):
-                h = raws[("w1", "w3")[n - 2], 1, 1][:, 0, :]
+            return bank
+
+        def features_end(n, bank):
+            if n == 3:
+                h = raws["w1", 1, 0][:, 0, :]
             else:
-                h = ring.tile([P, S], F32, name="h")[:]
+                h = ring.tile([P, S], F32, name="h", align_bytes=64)[:]
             nc.scalar.copy(h, bank[:])
             return h
 
         cos_x = [keep.tile([P, PACK, M], F32, name="cos_x%d" % b) for b in range(2)]
 
         def put(n, h):
-            nc.vector.tensor_tensor(pages[n % 2][:].indirect(list2[:]), h, wgs_sb[:], MULT)
+            nc.vector.tensor_tensor(pages[n % PAGES][:].indirect(list2[:]), h, wgs_sb[:], MULT)
+
+        def picked(n):
+            if n in (2, 3):
+                return shared[3][:, PASS * (n - 2):PASS * (n - 1)]
+            return limited_slice(n + 2) if n + 2 < 8 else cos_x[1][:, n % PACK, :]
 
         def pick(n, lo, hi):
-            b, i = divmod(n, PACK)
-            nc.vector.tensor_copy(cos_x[b][:, i, lo:hi], pages[n % 2][:].indirect(list3[:, lo // 16:hi // 16]))
+            nc.vector.tensor_copy(picked(n)[:, lo:hi], pages[n % PAGES][:].indirect(list3[:, lo // 16:hi // 16]))
 
         def cosine(n, lo, hi):
             b, i = divmod(n, PACK)
-            size = limited[1][:, min(max(n - 1, 0), 3)].rearrange("p j q -> p (j q)")[:, lo:hi]
-            nc.scalar.activation(size, cos_x[b][:, i, lo:hi], ACT.Abs)
+            size = spent[min(max(n + 3, 4), 7)][n % 2][:, 0:hi - lo]
+            nc.scalar.activation(size, picked(n)[:, lo:hi], ACT.Abs)
             nc.scalar.activation(cos_x[b][:, i, lo:hi], size, ACT.Sin, bias=math.pi / 2, scale=-1.0)
 
         z_w = [keep.tile([P, M], U32, name="z_w%d" % b, align_bytes=64) for b in range(2)]
         z_s = [keep.tile([P, M], U8, name="z_s%d" % b, align_bytes=64) for b in range(2)]
 
-        def quantise_z(b, lo, hi):
-            z = ring.tile([P, hi - lo, PACK], BF16, name="z", align_bytes=64, bufs=2)
+        def quantise_z(b, lo, hi, z=None):
+            if z is None:
+                z = ring.tile([P, hi - lo, PACK], BF16, name="z", align_bytes=64, bufs=1)
             nc.vector.tensor_tensor(
                 z[:].rearrange("p (c i) t -> p c t i", i=4),
                 cos_x[b][:, :, lo:hi].rearrange("p t (c i) -> p c t i", i=4),
@@ -238,6 +257,7 @@ def tile_list_vibrometer_slot_features_kernel(
 
         y_w = keep.tile([P, M], I32, name="y_w", align_bytes=64)
         y_s = keep.tile([P, M], U8, name="y_s", align_bytes=64)
+        y_bf = keep.tile([P, M, PACK], BF16, name="y_bf", align_bytes=64)
         out_rows = out_0.rearrange("(p t) m -> p t m", t=PACK)
         out_words = out_1[0].rearrange("p m t -> p (m t)").bitcast(I32)
 
@@ -246,48 +266,56 @@ def tile_list_vibrometer_slot_features_kernel(
             y = ring.tile([P, PACK, P], F32, name="y", bufs=4)
             nc.scalar.copy(y[:], y_banks[mq][:])
             nc.sync.dma_start(out_rows[:, :, cols], y[:])
-            y_bf = ring.tile([P, P, PACK], BF16, name="y_bf", align_bytes=64, bufs=2)
             nc.vector.tensor_copy(
-                y_bf[:].rearrange("p (c i) t -> p c t i", i=4), y[:].rearrange("p t (c i) -> p c t i", i=4))
-            nc.vector.quantize_mx(
-                out=y_w[:, cols].bitcast(FP8X4), scales=y_s[:, cols], in_=y_bf[:].rearrange("p m t -> p (m t)"))
-            nc.sync.dma_start(out_words[:, cols], y_w[:, cols])
+                y_bf[:, cols].rearrange("p (c i) t -> p c t i", i=4), y[:].rearrange("p t (c i) -> p c t i", i=4))
+            if mq % 2 == 1:
+                half = slice(P * (mq - 1), P * (mq + 1))
+                nc.vector.quantize_mx(
+                    out=y_w[:, half].bitcast(FP8X4), scales=y_s[:, half], in_=y_bf[:, half].rearrange("p m t -> p (m t)"))
+                nc.sync.dma_start(out_words[:, half], y_w[:, half])
 
-        quantise_chunk(("w1", 0, 0), [("scalar", 0, P)])
-        limited_features(0)
-        quantise_chunk(("w1", 0, 1), [("vector", 0, P)])
         quantise_chunk(("w3", 0, 0), [("vector", 0, P)])
-        quantise_chunk(("w3", 0, 1), [("vector", 0, P // 2), ("vector", P // 2, P)], (0, 1, PACK))
+        limited_features(0)
+        quantise_chunk(("w3", 0, 1), [("scalar", 0, P)])
+        quantise_chunk(("w1", 0, 0), [("vector", 0, P)])
+        quantise_chunk(("w1", 0, 1), [("vector", 0, P // 2), ("vector", P // 2, P)], (0, 1, PACK))
         limited_features(1)
-        second = [("w1", 1, 0), ("w1", 1, 1), ("w3", 1, 0), ("w3", 1, 1)]
-        hs = {0: features(0)}
+        second = [("w3", 1, 0), ("w3", 1, 1), ("w1", 1, 0), ("w1", 1, 1)]
+        hs = {0: features(0), 1: features(1)}
         deal_w4()
-        for n in range(8):
-            if n in (1, 2):
-                quantise_chunk(second[2 * n - 2], [("scalar", 0, P)])
-                quantise_chunk(second[2 * n - 1], [("scalar", 0, P)])
-            if n + 1 < 8:
-                hs[n + 1] = features(n + 1)
-            if n == 3:
+        put(0, hs[0])
+        hs[2] = features(2)
+        for n in range(1, 8):
+            if n == 1:
+                start3 = features_start(3)
+                for key in second[:3]:
+                    quantise_chunk(key, [("scalar", 0, P)])
+                hs[3] = features_end(3, start3)
+                quantise_chunk(second[3], [("scalar", 0, P)])
+            elif n + 2 < 8:
+                hs[n + 2] = features(n + 2)
+            if n == 2:
                 cosine(0, 0, M)
-            if n >= 3 and n < 6:
+            if 3 <= n < 6:
                 cosine(n - 2, 0, M)
             if n == 5:
-                quantise_z(0, 0, M)
+                quantise_z(0, 0, M // 2)
             put(n, hs[n])
-            if n < 7:
-                pick(n, 0, M)
+            pick(n - 1, 0, M)
         for n in range(4, 7):
             cosine(n, 0, M)
-        for mq in range(4):
+        for mq in range(2):
             project(0, mq)
         for half in range(2):
             pick(7, 256 * half, 256 * (half + 1))
             cosine(7, 256 * half, 256 * (half + 1))
-        for half in range(2):
-            quantise_z(1, 256 * half, 256 * (half + 1))
-            for mq in (2 * half, 2 * half + 1):
-                project(1, mq)
+        quantise_z(0, M // 2, M, hs[7].bitcast(BF16).rearrange("p (m t) -> p m t", t=PACK))
+        quantise_z(1, 0, M // 2)
+        for b, mq in ((1, 0), (1, 1), (0, 2), (0, 3)):
+            project(b, mq)
+        quantise_z(1, M // 2, M)
+        for mq in (2, 3):
+            project(1, mq)
         for mq in range(4):
             hand_out(mq)
         for q in range(QUADS):

@@ -145,7 +145,9 @@ def tile_list_vibrometer_slot_features_kernel(
             src = raw[:].rearrange("p t (q i) -> p q t i", i=PACK)
             for engine, lo, hi in shares:
                 if engine == "vector":
-                    nc.vector.tensor_copy(dst[:, lo:hi], src[:, lo:hi])
+                    nc.vector.tensor_copy(
+                        grouped.rearrange("p (u i) q t -> p u q t i", u=2)[:, :, lo:hi],
+                        raw[:].rearrange("p t (q u i) -> p u q t i", u=2, i=2)[:, :, lo:hi])
                 else:
                     nc.scalar.copy(dst[:, lo:hi], src[:, lo:hi])
             label = "%s%d%d" % key
@@ -238,9 +240,9 @@ def tile_list_vibrometer_slot_features_kernel(
 
         def deal_w4():
             nc.vector.tensor_copy(
-                w4_wd[:].rearrange("p a (t q) -> p a q t", t=PACK), w4_w[:].rearrange("p a (q t) -> p a q t", t=PACK))
+                w4_wd[:].rearrange("p a (u t q) -> p a u q t", u=2, t=2), w4_w[:].rearrange("p a (q u t) -> p a u q t", u=2, t=2))
             nc.vector.tensor_copy(
-                w4_sd[:].rearrange("p (t q) -> p q t", t=PACK), w4_s[:].rearrange("p (q t) -> p q t", t=PACK))
+                w4_sd[:].rearrange("p (u t q) -> p u q t", u=2, t=2), w4_s[:].rearrange("p (q u t) -> p u q t", u=2, t=2))
 
         y_banks = {}
 

import math
from contextlib import ExitStack

import concourse.mybir as mybir
from concourse.masks import make_identity

K, T, S, H, T2, M, N = 1024, 2048, 512, 1024, 1024, 512, 512
FLOPS = 2 * (3 * K * H * S + H * N * M)

F32 = mybir.dt.float32
BF16 = mybir.dt.bfloat16
I32 = mybir.dt.int32
U32 = mybir.dt.uint32
U16 = mybir.dt.uint16
U8 = mybir.dt.uint8
FP8X4 = mybir.dt.float8_e4m3fn_x4
FP4X4 = mybir.dt.float4_e2m1fn_x4
ACT = mybir.ActivationFunctionType
MULT = mybir.AluOpType.mult

P = 128
PACK = 4
PASS = P * PACK
QUADS = 4
PAGES = 3


def tile_list_vibrometer_slot_features_kernel(
    tc, tab_words, tab_scales, offs, w1, w2_words, w2_scales, w3, amp, wgs, offs2, offs3, geo,
    w4_words, w4_scales, out_0, out_1, out_2,
):
    nc = tc.nc
    with ExitStack() as ctx:
        keep = ctx.enter_context(tc.tile_pool(name="keep", bufs=1))
        big = ctx.enter_context(tc.tile_pool(name="big", bufs=7))
        ring = ctx.enter_context(tc.tile_pool(name="ring", bufs=3))
        psum = ctx.enter_context(tc.psum_pool(name="psum", bufs=2))

        list1 = keep.tile([P, S // 16], U16, name="list1")
        list2 = keep.tile([P, S // 16], U16, name="list2")
        list3 = keep.tile([P, M // 16], U16, name="list3")
        tab_s = keep.tile([P, 2 * T], U8, name="tab_s", align_bytes=64)
        w2_s = keep.tile([P, 2 * H], U8, name="w2_s", align_bytes=64)
        w4_s = keep.tile([P, N], U8, name="w4_s", align_bytes=64)
        nc.vector.memset(tab_s[:].bitcast(I32), 0)
        nc.vector.memset(w2_s[:].bitcast(I32), 0)
        nc.vector.memset(w4_s[:].bitcast(I32), 0)
        pages = [keep.tile([P, T2], F32, name="page%d" % n) for n in range(PAGES)]
        for page in pages:
            nc.vector.memset(page[:], 0.0)
        ident = keep.tile([P, P], F32, name="ident")
        make_identity(nc, ident[:])

        nc.sync.dma_start(list1[:], offs)
        tab_w = [keep.tile([P, T], I32, name="tab_w%d" % a, align_bytes=64) for a in range(2)]

        def load_scales(dst, src):
            for q in range(QUADS):
                nc.sync.dma_start(
                    dst[32 * q:32 * q + 4, :].bitcast(I32).rearrange("r (a n) -> r a n", a=2),
                    src[:, 4 * q:4 * q + 4, :].bitcast(I32).rearrange("a r n -> r a n"),
                )

        def load_chunk(w, b, a, pieces=1):
            raw = big.tile([P, PACK, PASS], F32, name="raw", tag="big")
            rows = w[PASS * a:PASS * (a + 1), PASS * b:PASS * (b + 1)].rearrange("(p t) c -> p t c", t=PACK)
            width = PASS // pieces
            for lo in range(0, PASS, width):
                nc.sync.dma_start(raw[:, :, lo:lo + width], rows[:, :, lo:lo + width])
            return raw

        def load_table(a):
            nc.sync.dma_start(tab_w[a][:], tab_words[a].rearrange("p t i -> p (t i)").bitcast(I32))

        raws = {}
        amp_col = keep.tile([P, 2, PACK], F32, name="amp_col")
        nc.sync.dma_start(amp_col[:], amp.rearrange("(b q i) -> q b i", b=2, i=PACK))
        load_table(0)
        load_scales(tab_s, tab_scales)
        load_table(1)
        w2_w = keep.tile([P, 2, 2 * H], U8, name="w2_w", align_bytes=64)
        nc.sync.dma_start(w2_w[:].bitcast(I32), w2_words.bitcast(I32).rearrange("a p n -> p a n"))
        load_scales(w2_s, w2_scales)
        raws["w3", 0, 0] = load_chunk(w3, 0, 0)
        raws["w3", 0, 1] = load_chunk(w3, 0, 1)
        raws["w1", 0, 0] = load_chunk(w1, 0, 0)
        raws["w1", 0, 1] = load_chunk(w1, 0, 1, 2)
        wgs_sb = keep.tile([P, S], F32, name="wgs_sb")
        nc.sync.dma_start(list2[:], offs2)
        nc.sync.dma_start(wgs_sb[:], wgs)
        nc.sync.dma_start(list3[:], offs3)
        for name, w in (("w3", w3), ("w1", w1)):
            for a in range(2):
                raws[name, 1, a] = load_chunk(w, 1, a)
        w4_w = keep.tile([P, 2, N], I32, name="w4_w", align_bytes=64)
        nc.sync.dma_start(w4_w[:], w4_words.rearrange("a p c i -> p a (c i)").bitcast(I32))
        for q in range(QUADS):
            nc.sync.dma_start(
                w4_s[32 * q:32 * q + 8, :].bitcast(I32), w4_scales[:, 4 * q:4 * q + 4, :].bitcast(I32))
        geo_sb = []
        for b in range(2):
            g = big.tile([P, PACK, M], F32, name="geo%d" % b, tag="big")
            nc.sync.dma_start(g[:], geo[PASS * b:PASS * (b + 1), :].rearrange("(p t) m -> p t m", t=PACK))
            geo_sb.append(g)

        v_s = [keep.tile([P, S], U8, name="v_s%d" % a, align_bytes=64) for a in range(2)]
        v_w = [keep.tile([P, S], U32, name="v_w%d" % a, align_bytes=64) for a in range(2)]
        for a in range(2):
            nc.vector.tensor_copy(v_s[a][:], tab_s[:, T * a:T * (a + 1)].indirect(list1[:]))
            nc.vector.tensor_copy(v_w[a][:], tab_w[a][:].bitcast(U32).indirect(list1[:]))

        amp_row = []
        for b in range(2):
            bank = psum.tile([P, PASS], F32, name="amp_row", tag="amp")
            for i in range(PACK):
                nc.tensor.transpose(bank[:, P * i:P * (i + 1)], amp_col[:, b, i:i + 1].to_broadcast([P, P]), ident[:])
            amp_row.append(bank)

        tanhs = [keep.tile([P, PACK, 4, P], F32, name="tanh%d" % b) for b in range(2)]
        limited = [tanhs[0][:], raws["w1", 0, 1][:].rearrange("p i (j q) -> p i j q", j=4)]

        def limited_features(b):
            banks = [psum.tile([P, PASS], F32, name="bank", tag="mx", bufs=4) for jb in range(4)]
            for jb in range(4):
                for a in range(2):
                    cols = slice(P * jb, P * (jb + 1))
                    nc.tensor.matmul_mx(
                        out=banks[jb][:], lhsT=v_w[a][:, cols].bitcast(FP8X4), lhsT_scale=v_s[a][:, cols],
                        rhs=w2_w[:, a, 2 * PASS * b:2 * PASS * (b + 1)].bitcast(FP4X4),
                        rhs_scale=w2_s[:, H * a + PASS * b:H * a + PASS * (b + 1)],
                        start=(a == 0), stop=(a == 1))
            for jb, bank in enumerate(banks):
                nc.scalar.activation(tanhs[b][:, :, jb, :], bank[:].rearrange("p (q i) -> p i q", i=PACK), ACT.Tanh)
                nc.vector.tensor_tensor(
                    limited[b][:, :, jb, :], tanhs[b][:, :, jb, :], amp_row[b][:].rearrange("p (i q) -> p i q", i=PACK), MULT)

        codes, scales = {}, {}
        shared = [keep.tile([P, 2 * PASS], F32, name="shared%d" % n, align_bytes=64) for n in range(4)]

        def quantise_chunk(key, shares, cuts=(0, PACK)):
            raw = raws[key]
            place = shared[2 * (key[0] == "w1") + key[2]]
            grouped = place[:].bitcast(BF16).rearrange("p (i q t) -> p i q t", i=PACK, t=PACK)
            dst = grouped[:].rearrange("p i q t -> p q t i")
            src = raw[:].rearrange("p t (q i) -> p q t i", i=PACK)
            for engine, lo, hi in shares:
                if engine == "vector":
                    nc.vector.tensor_copy(
                        grouped.rearrange("p (u i) q t -> p u q t i", u=2)[:, :, lo:hi],
                        raw[:].rearrange("p t (q u i) -> p u q t i", u=2, i=2)[:, :, lo:hi])
                else:
                    nc.scalar.copy(dst[:, lo:hi], src[:, lo:hi])
            label = "%s%d%d" % key
            codes[key] = keep.tile([P, PASS], U32, name="c" + label, align_bytes=64)
            scales[key] = keep.tile([P, PASS], U8, name="s" + label, align_bytes=64)
            for lo, hi in zip(cuts, cuts[1:]):
                nc.vector.quantize_mx(
                    out=codes[key][:, P * lo:P * hi].bitcast(FP8X4), scales=scales[key][:, P * lo:P * hi],
                    in_=grouped[:, lo:hi].rearrange("p i q t -> p (i q t)"))

        def product(name, b, i):
            bank = psum.tile([P, PASS], F32, name="bank", tag="mx", bufs=4)
            rows = slice(P * i, P * (i + 1))
            for a in range(2):
                for jb in range(4):
                    cols = slice(P * jb, P * (jb + 1))
                    nc.tensor.matmul_mx(
                        out=bank[:, cols], lhsT=v_w[a][:, cols].bitcast(FP8X4), lhsT_scale=v_s[a][:, cols],
                        rhs=codes[name, b, a][:, rows].bitcast(FP8X4), rhs_scale=scales[name, b, a][:, rows],
                        start=(a == 0 and jb == 0), stop=(a == 1 and jb == 3))
            return bank

        spent = {}

        def limited_slice(n):
            return limited[n // PACK][:, n % PACK].rearrange("p j q -> p (j q)")

        def features(n):
            return features_end(n, features_start(n))

        def features_start(n):
            b, i = divmod(n, PACK)
            phase = ring.tile([P, PASS], F32, name="phase")
            plain = shared[n][:, 0:PASS] if n < PACK else ring.tile([P, PASS], F32, name="plain")
            spent[n] = (phase, plain)
            nc.scalar.activation(phase[:], product("w3", b, i)[:], ACT.Sin)
            nc.scalar.copy(plain[:], product("w1", b, i)[:])
            bank = psum.tile([P, S], F32, name="hsum", tag="hsum")
            terms = (limited_slice(n), phase[:], plain[:]) if n % PACK < 2 else (phase[:], plain[:], limited_slice(n))
            for k, term in enumerate(terms):
                for jb in range(4):
                    cols = slice(P * jb, P * (jb + 1))
                    nc.tensor.matmul(
                        bank[:, cols], term[:, cols], ident[:], start=(k == 0 and jb == 0), stop=(k == 2 and jb == 3),
                        is_transpose=True)
            return bank

        def features_end(n, bank):
            if n == 3:
                h = raws["w1", 1, 0][:, 0, :]
            else:
                h = ring.tile([P, S], F32, name="h", align_bytes=64)[:]
            nc.scalar.copy(h, bank[:])
            return h

        cos_x = [keep.tile([P, PACK, M], F32, name="cos_x%d" % b) for b in range(2)]

        def put(n, h):
            nc.vector.tensor_tensor(pages[n % PAGES][:].indirect(list2[:]), h, wgs_sb[:], MULT)

        def picked(n):
            if n in (2, 3):
                return shared[3][:, PASS * (n - 2):PASS * (n - 1)]
            return limited_slice(n + 2) if n + 2 < 8 else cos_x[1][:, n % PACK, :]

        def pick(n, lo, hi):
            nc.vector.tensor_copy(picked(n)[:, lo:hi], pages[n % PAGES][:].indirect(list3[:, lo // 16:hi // 16]))

        def cosine(n, lo, hi):
            b, i = divmod(n, PACK)
            size = spent[min(max(n + 3, 4), 7)][n % 2][:, 0:hi - lo]
            nc.scalar.activation(size, picked(n)[:, lo:hi], ACT.Abs)
            nc.scalar.activation(cos_x[b][:, i, lo:hi], size, ACT.Sin, bias=math.pi / 2, scale=-1.0)

        z_w = [keep.tile([P, M], U32, name="z_w%d" % b, align_bytes=64) for b in range(2)]
        z_s = [keep.tile([P, M], U8, name="z_s%d" % b, align_bytes=64) for b in range(2)]

        def quantise_z(b, lo, hi, z=None):
            if z is None:
                z = ring.tile([P, hi - lo, PACK], BF16, name="z", align_bytes=64, bufs=1)
            nc.vector.tensor_tensor(
                z[:].rearrange("p (c i) t -> p c t i", i=4),
                cos_x[b][:, :, lo:hi].rearrange("p t (c i) -> p c t i", i=4),
                geo_sb[b][:, :, lo:hi].rearrange("p t (c i) -> p c t i", i=4), MULT)
            nc.vector.quantize_mx(
                out=z_w[b][:, lo:hi].bitcast(FP8X4), scales=z_s[b][:, lo:hi], in_=z[:].rearrange("p m t -> p (m t)"))

        w4_wd = keep.tile([P, 2, N], I32, name="w4_wd", align_bytes=64)
        w4_sd = keep.tile([P, N], U8, name="w4_sd", align_bytes=64)

        def deal_w4():
            nc.vector.tensor_copy(
                w4_wd[:].rearrange("p a (u t q) -> p a u q t", u=2, t=2), w4_w[:].rearrange("p a (q u t) -> p a u q t", u=2, t=2))
            nc.vector.tensor_copy(
                w4_sd[:].rearrange("p (u t q) -> p u q t", u=2, t=2), w4_s[:].rearrange("p (q u t) -> p u q t", u=2, t=2))

        y_banks = {}

        def project(b, mq):
            if b == 0:
                y_banks[mq] = psum.tile([P, PACK, P], F32, name="bank", tag="mx", bufs=4)
            cols = slice(P * mq, P * (mq + 1))
            for t in range(PACK):
                rows = slice(P * t, P * (t + 1))
                nc.tensor.matmul_mx(
                    out=y_banks[mq][:, t, :], lhsT=w4_wd[:, b, rows].bitcast(FP8X4), lhsT_scale=w4_sd[4 * b:P, rows],
                    rhs=z_w[b][:, cols].bitcast(FP8X4), rhs_scale=z_s[b][:, cols],
                    start=(b == 0 and t == 0), stop=(b == 1 and t == PACK - 1))

        y_w = keep.tile([P, M], I32, name="y_w", align_bytes=64)
        y_s = keep.tile([P, M], U8, name="y_s", align_bytes=64)
        y_bf = keep.tile([P, M, PACK], BF16, name="y_bf", align_bytes=64)
        out_rows = out_0.rearrange("(p t) m -> p t m", t=PACK)
        out_words = out_1[0].rearrange("p m t -> p (m t)").bitcast(I32)

        def hand_out(mq):
            cols = slice(P * mq, P * (mq + 1))
            y = ring.tile([P, PACK, P], F32, name="y", bufs=4)
            nc.scalar.copy(y[:], y_banks[mq][:])
            nc.sync.dma_start(out_rows[:, :, cols], y[:])
            nc.vector.tensor_copy(
                y_bf[:, cols].rearrange("p (c i) t -> p c t i", i=4), y[:].rearrange("p t (c i) -> p c t i", i=4))
            if mq % 2 == 1:
                half = slice(P * (mq - 1), P * (mq + 1))
                nc.vector.quantize_mx(
                    out=y_w[:, half].bitcast(FP8X4), scales=y_s[:, half], in_=y_bf[:, half].rearrange("p m t -> p (m t)"))
                nc.sync.dma_start(out_words[:, half], y_w[:, half])

        quantise_chunk(("w3", 0, 0), [("vector", 0, P)])
        limited_features(0)
        quantise_chunk(("w3", 0, 1), [("scalar", 0, P)])
        quantise_chunk(("w1", 0, 0), [("vector", 0, P)])
        quantise_chunk(("w1", 0, 1), [("vector", 0, P // 2), ("vector", P // 2, P)], (0, 1, PACK))
        limited_features(1)
        second = [("w3", 1, 0), ("w3", 1, 1), ("w1", 1, 0), ("w1", 1, 1)]
        hs = {0: features(0), 1: features(1)}
        deal_w4()
        put(0, hs[0])
        hs[2] = features(2)
        for n in range(1, 8):
            if n == 1:
                start3 = features_start(3)
                for key in second[:3]:
                    quantise_chunk(key, [("scalar", 0, P)])
                hs[3] = features_end(3, start3)
                quantise_chunk(second[3], [("scalar", 0, P)])
            elif n + 2 < 8:
                hs[n + 2] = features(n + 2)
            if n == 2:
                cosine(0, 0, M)
            if 3 <= n < 6:
                cosine(n - 2, 0, M)
            if n == 5:
                quantise_z(0, 0, M // 2)
            put(n, hs[n])
            pick(n - 1, 0, M)
        for n in range(4, 7):
            cosine(n, 0, M)
        for mq in range(2):
            project(0, mq)
        for half in range(2):
            pick(7, 256 * half, 256 * (half + 1))
            cosine(7, 256 * half, 256 * (half + 1))
        quantise_z(0, M // 2, M, hs[7].bitcast(BF16).rearrange("p (m t) -> p m t", t=PACK))
        quantise_z(1, 0, M // 2)
        for b, mq in ((1, 0), (1, 1), (0, 2), (0, 3)):
            project(b, mq)
        quantise_z(1, M // 2, M)
        for mq in (2, 3):
            project(1, mq)
        for mq in range(4):
            hand_out(mq)
        for q in range(QUADS):
            nc.scalar.dma_start(out_2[0, 4 * q:4 * q + 4, :].bitcast(I32), y_s[32 * q:32 * q + 4, :].bitcast(I32))
